import numpy as np
import ml_dtypes


def mxq(x, axis, fmt="e4m3"):
    dtype, down = {"e4m3": (ml_dtypes.float8_e4m3fn, 7), "e5m2": (ml_dtypes.float8_e5m2, 14)}[fmt]
    v = np.moveaxis(np.asarray(x, np.float32).astype(ml_dtypes.bfloat16).astype(np.float64), axis, -1)
    blocks = v.reshape(v.shape[:-1] + (-1, 32))
    amax = np.abs(blocks).max(-1, keepdims=True)
    byte = np.maximum(np.where(amax > 0, np.frexp(amax)[1] - 1 + 127, 0) - down, 1)
    scale = np.exp2(byte - 127.0)
    codes = (blocks / scale).astype(np.float32).astype(dtype).astype(np.float64)
    return np.moveaxis((codes * scale).reshape(v.shape), -1, axis)


WIDE = False


def mx_kscale(k):
    if not WIDE:
        return np.ones(k)
    levels = np.array([10, -10, 5, -5, 0])
    if k % 512:
        return np.exp2(np.random.permutation(np.resize(levels, k // 32))).repeat(32)
    a = np.empty((k // 512, 16))
    for p in range(k // 512):
        a[p, :8] = np.random.permutation(np.resize(levels, 8))
        for g in range(8):
            far = levels[np.abs(levels - a[p, g]) >= 10]
            a[p, g + 8] = far[np.random.randint(len(far))]
    return np.exp2(a.ravel()).repeat(32)


def f64(x):
    return np.asarray(x).astype(np.float64)


def striped(idx):
    return np.tile(idx.reshape(-1, 16).T, (8, 1)).astype(np.uint16)


def unstriped(offs):
    return offs[:16].T.reshape(-1).astype(np.int64)


E2M1 = np.array([0.0, 0.5, 1.0, 1.5, 2.0, 3.0, 4.0, 6.0, -0.0, -0.5, -1.0, -1.5, -2.0, -3.0, -4.0, -6.0])


def pack_weight(w, fmt):
    k, n = w.shape
    w = f64(np.asarray(w, np.float32).astype(ml_dtypes.bfloat16)).reshape(k // 32, 32, n)
    amax = np.abs(w).max(1)
    if fmt == "e4m3":
        byte = np.frexp(amax)[1] - 1 + 127 - 7
    else:
        mant, ex = np.frexp(amax / 6.0)
        byte = np.where(mant > 0.5, ex, ex - 1) + 127
    byte = np.clip(np.where(amax > 0, byte, 1), 1, 254)
    scaled = (w * np.exp2(127.0 - byte)[:, None, :]).reshape(k, n).astype(np.float32)
    by_word = np.ascontiguousarray(scaled.reshape(k // 512, 128, 4, n).transpose(0, 1, 3, 2))
    if fmt == "e4m3":
        words = by_word.astype(ml_dtypes.float8_e4m3fn).view(np.uint8)
    else:
        c = by_word.astype(ml_dtypes.float4_e2m1fn).view(np.uint8) & 0xF
        words = (c[..., 0::2] | (c[..., 1::2] << 4)).reshape(k // 512, 128, 2 * n)
    return np.ascontiguousarray(words), np.ascontiguousarray(byte.astype(np.uint8).reshape(k // 512, 16, n))


def unpack_weight(words, scales, fmt):
    g, _, n = scales.shape
    words = np.ascontiguousarray(words).reshape(g, 128, n, -1)
    if fmt == "e4m3":
        vals = words.view(ml_dtypes.float8_e4m3fn).astype(np.float64)
    else:
        nib = np.empty((g, 128, n, 4), np.uint8)
        nib[..., 0::2] = words & 0xF
        nib[..., 1::2] = words >> 4
        vals = E2M1[nib]
    vals = vals * np.repeat(np.exp2(scales.astype(np.float64) - 127.0), 8, axis=1)[..., None]
    return vals.transpose(0, 1, 3, 2).reshape(g * 512, n)


def gelu(v):
    return 0.5 * v * (1.0 + np.tanh(np.sqrt(2.0 / np.pi) * (v + 0.044715 * v**3)))


K, T, S, H, T2, P, D, N = 1024, 4096, 1024, 512, 2048, 512, 512, 256

def setup_inputs():
    n = np.random.standard_normal
    s = mx_kscale(K)[:, None]
    u = mx_kscale(H)[:, None]
    d = mx_kscale(D)[:, None]
    tab_words, tab_scales = pack_weight(n((K, T)) * s, "e4m3")
    w3_words, w3_scales = pack_weight(n((K, H)) / np.sqrt(K) / s, "e4m3")
    w4_words, w4_scales = pack_weight(0.7 * n((H, N)) / np.sqrt(H) / u, "e2m1")
    perm = np.random.permutation(T2)
    return {
        "tab_words": tab_words, "tab_scales": tab_scales,
        "offs": striped(np.random.permutation(T)[:S]),
        "offs2": striped(np.random.permutation(T2)[:S]),
        "offs3": striped(perm[:P]),
        "offs4": striped(perm[P:2 * P]),
        "w1": (n((K, H)) / np.sqrt(K) / s).astype(np.float32),
        "w2": (n((K, H)) / np.sqrt(K) / s).astype(np.float32),
        "w3_words": w3_words, "w3_scales": w3_scales,
        "gain": (np.exp(0.3 * n(H)) * u[:, 0]).astype(np.float32),
        "wgs": np.exp(0.3 * n((128, S))).astype(np.float32),
        "page0": (n((H, T2)) * u).astype(np.float32),
        "w4_words": w4_words, "w4_scales": w4_scales,
        "ctx": (n((D, T2)) * d).astype(np.float32),
        "w5": (0.8 * n((D, N)) / np.sqrt(D) / d).astype(np.float32),
    }

def reference(tab_words, tab_scales, offs, offs2, offs3, offs4, w1, w2, w3_words, w3_scales, gain, wgs, page0, w4_words, w4_scales, ctx, w5):
    v = unpack_weight(tab_words, tab_scales, "e4m3")[:, unstriped(offs)]
    b1 = mxq(f64(w1), 0, "e4m3").T @ v
    b2 = mxq(f64(w2), 0, "e4m3").T @ v
    b3 = unpack_weight(w3_words, w3_scales, "e4m3").T @ v
    h = f64(gain)[:, None] * (np.maximum(b1, b2) + b3)
    page = f64(page0).copy()
    page[:, unstriped(offs2)] = np.tile(f64(wgs), (H // 128, 1)) * h
    a = page[:, unstriped(offs3)]
    b = page[:, unstriped(offs4)]
    page[:, unstriped(offs3)] = np.maximum(a, b)
    page[:, unstriped(offs4)] = a + b
    w4 = unpack_weight(w4_words, w4_scales, "e2m1")
    y = w4.T @ mxq(page, 0, "e4m3") + mxq(f64(w5), 0, "e4m3").T @ mxq(f64(ctx), 0, "e4m3")
    return np.tanh(y)

from contextlib import ExitStack

import concourse.mybir as mybir
from concourse.masks import make_identity

K, T, S, H, T2, PAIRS, D, N = 1024, 4096, 1024, 512, 2048, 512, 512, 256
FLOPS = 2 * (3 * K * H * S + H * N * T2 + D * N * T2)

F32 = mybir.dt.float32
BF16 = mybir.dt.bfloat16
I32 = mybir.dt.int32
U32 = mybir.dt.uint32
U16 = mybir.dt.uint16
U8 = mybir.dt.uint8
FP8X4 = mybir.dt.float8_e4m3fn_x4
FP4X4 = mybir.dt.float4_e2m1fn_x4
ALU = mybir.AluOpType
ACT = mybir.ActivationFunctionType

P = 128
PASSES = K // 512
BANK = 512
SLICES = [((0, 256), (256, 512), (512, 1024))] + [((0, 512), (512, 1024))] * 3
HALF = H // 2
PIECE = 256
OUT_COLS = 256
SCALAR_CHUNKS = 3


def tile_list_placement_bid_shading_kernel(
    tc, tab_words, tab_scales, offs, offs2, offs3, offs4, w1, w2, w3_words, w3_scales,
    gain, wgs, page0, w4_words, w4_scales, ctx, w5, out,
):
    nc = tc.nc
    with ExitStack() as stack:
        stack.enter_context(nc.allow_non_contiguous_dma(reason="gain: one value a partition"))
        keep = stack.enter_context(tc.tile_pool(name="keep", bufs=1))
        ring = stack.enter_context(tc.tile_pool(name="ring", bufs=2))
        raws = stack.enter_context(tc.tile_pool(name="raws", bufs=8))
        psum = stack.enter_context(tc.psum_pool(name="psum", bufs=2))

        def kept(name, shape, dtype):
            return keep.tile(shape, dtype, name=name, align_bytes=64)

        lists = [kept("list1", [P, S // 16], U16), kept("list2", [P, S // 16], U16),
                 kept("list3", [P, PAIRS // 16], U16), kept("list4", [P, PAIRS // 16], U16)]
        tab = [kept("tab%d" % a, [P, T], I32) for a in range(PASSES)]
        tab_plane = kept("tab_plane", [P, T], U8)
        v = [kept("v%d" % a, [P, S], U32) for a in range(PASSES)]
        v_plane = kept("v_plane", [P, S], U8)
        w3_raw = kept("w3_raw", [P, PASSES, H], I32)
        w3_raw_plane = kept("w3_raw_plane", [P, H], U8)
        w3c = kept("w3c", [P, PASSES, H], I32)
        w3_plane = kept("w3_plane", [P, H], U8)
        w_in_a = kept("w_in_a", [P, 4 * P * 4], BF16)
        w_in_b = kept("w_in_b", [P, 4 * P * 2], F32)
        w_in_cd = kept("w_in_cd", [P, 2, 4 * P * 4], BF16)
        w12c = kept("w12c", [P, 4 * P], U32)
        w_plane = kept("w_plane", [P, 4 * P], U8)
        w5_raw = kept("w5_raw", [P, 4, N], F32)
        w5_in = kept("w5_in", [P, N * 4], BF16)
        w5c = kept("w5c", [P, N], U32)
        w4c = kept("w4c", [P, 2 * N], U8)
        w4_plane = kept("w4_plane", [P, N], U8)
        pages = [kept("page%d" % t, [P, T2], F32) for t in range(4)]
        gain_ab = kept("gain_ab", [P, 2], F32)
        gain_cd = kept("gain_cd", [P, 2], F32)
        ident = kept("ident", [P, P], F32)
        first = kept("first", [P, PAIRS], F32)
        second = w_in_b[:, 0:PAIRS]
        spare = kept("spare", [P, S], F32)
        b3s = kept("b3s", [P, S], F32)
        mh = kept("mh", [P, S], F32)
        rounded = kept("rounded", [P, T2], BF16)
        planes3 = kept("planes3", [P, 3, T2], BF16)
        last_in = [kept("last_in%d" % c, [P, 2, OUT_COLS, 4], BF16) for c in range(T2 // OUT_COLS)]

        nc.vector.memset(tab_plane[:].bitcast(I32), 0)
        for q in range(4):
            nc.scalar.dma_start(out=tab_plane[32 * q : 32 * q + 8, :].bitcast(I32),
                                in_=tab_scales[:, 4 * q : 4 * q + 4, :].bitcast(I32))
        nc.vector.memset(w3_raw_plane[:].bitcast(I32), 0)
        for q in range(4):
            nc.scalar.dma_start(out=w3_raw_plane[32 * q : 32 * q + 8, :].bitcast(I32),
                                in_=w3_scales[:, 4 * q : 4 * q + 4, :].bitcast(I32))
        make_identity(nc, ident[:])
        gain_rows = gain.rearrange("(h q t) -> q t h", h=2, t=4)
        for e in range(2):
            nc.gpsimd.dma_start(out=gain_ab[e:P:2, :], in_=gain_rows[:, e, :])
        nc.gpsimd.dma_start(out=gain_cd[:], in_=gain.rearrange("(p t) -> p t", t=4)[:, 2:4])
        nc.gpsimd.memset(w4_plane[:].bitcast(I32), 0)
        for q in range(4):
            nc.gpsimd.dma_start(out=w4_plane[32 * q : 32 * q + 4, :].bitcast(I32),
                                in_=w4_scales[0, 4 * q : 4 * q + 4, :].bitcast(I32))

        def load_tab(a):
            nc.sync.dma_start(out=tab[a][:], in_=tab_words[a].rearrange("p n t -> p (n t)").bitcast(I32))

        def load_piece(src, a, col):
            raw = raws.tile([P, 4, PIECE], F32, name="raw", align_bytes=64)
            rows = src[512 * a : 512 * (a + 1), col : col + PIECE]
            nc.sync.dma_start(out=raw[:], in_=rows.rearrange("(p j) c -> p j c", j=4))
            return raw

        def load_w_half(h):
            return [load_piece(w, a, h * HALF) for a in range(PASSES) for w in (w1, w2)]

        def load_page(t):
            if t < 2:
                rows = page0[HALF * t : HALF * (t + 1), :].rearrange("(q t) c -> q t c", t=4)[:, 0:2, :]
            else:
                rows = page0.rearrange("(p t) c -> p t c", t=4)[:, t, :]
            nc.sync.dma_start(out=pages[t][:], in_=rows)

        def load_wgs(dealt, t, lo, hi):
            rows = wgs.rearrange("(q t) c -> q t c", t=4)
            if t < 2:
                for u in range(2):
                    nc.sync.dma_start(out=dealt[64 * u : 64 * (u + 1), lo:hi], in_=rows[:, 0:2, lo:hi])
            else:
                for u in range(4):
                    nc.sync.dma_start(out=dealt[32 * u : 32 * (u + 1), lo:hi], in_=rows[:, t, lo:hi])

        load_tab(0)
        for tile, src in zip(lists, (offs, offs2, offs3, offs4)):
            nc.sync.dma_start(tile[:], src)
        load_tab(1)
        raw0 = load_w_half(0)
        nc.sync.dma_start(out=w3_raw[:], in_=w3_words.rearrange("a p n t -> p a (n t)").bitcast(I32))
        dealt = ring.tile([P, S], F32, name="dealt")
        wgs_of = {0: dealt, 1: dealt}
        load_wgs(dealt, 0, *SLICES[0][0])
        load_page(0)
        load_wgs(dealt, 0, SLICES[0][0][1], S)
        raw1 = load_w_half(1)
        nc.sync.dma_start(out=w5_raw[:], in_=w5.rearrange("(p j) c -> p j c", j=4))
        load_page(1)

        nc.vector.tensor_copy(v[0][:], tab[0][:].bitcast(U32).indirect(lists[0][:]))
        nc.vector.tensor_copy(v_plane[:], tab_plane[:].indirect(lists[0][:]))
        nc.vector.tensor_copy(v[1][:], tab[1][:].bitcast(U32).indirect(lists[0][:]))

        def round_ab(copy, dst, raw, slot):
            copy(out=dst[:, 512 * slot : 512 * (slot + 1)].rearrange("p (q e j) -> p q e j", e=2, j=4),
                 in_=raw[:].rearrange("p j (q t) -> p q t j", t=4)[:, :, 0:2, :])

        def round_cd(raw, slot, h):
            at = 512 * slot + 256 * h
            nc.scalar.copy(out=w_in_cd[:, :, at : at + 256].rearrange("p e (q j) -> p e q j", j=4),
                           in_=raw[:].rearrange("p j (q t) -> p t q j", t=4)[:, 2:4, :, :])

        def quantise_w(src, lo, hi):
            nc.vector.quantize_mx(out=w12c[:, lo:hi].bitcast(FP8X4), scales=w_plane[:, lo:hi], in_=src[:, 4 * lo : 4 * hi])

        for a in range(PASSES):
            for w in range(2):
                round_ab(nc.vector.tensor_copy, w_in_a[:], raw0[2 * a + w], 2 * a + w)
            quantise_w(w_in_a, 256 * a, 256 * (a + 1))

        words = w3_raw[:].rearrange("p a (m t) -> p a m t", t=4)
        nc.vector.tensor_copy(out=w3c[:, :, 0:HALF].rearrange("p a (m e) -> p a m e", e=2), in_=words[:, :, :, 0:2])
        sbytes = w3_raw_plane[:].rearrange("p (m t) -> p m t", t=4)
        nc.vector.tensor_copy(out=w3_plane[:, 0:HALF].rearrange("p (m e) -> p m e", e=2), in_=sbytes[:, :, 0:2])
        nc.vector.tensor_copy(out=w3c[:, :, HALF:H].rearrange("p a (e m) -> p a e m", e=2),
                              in_=w3_raw[:].rearrange("p a (m t) -> p a t m", t=4)[:, :, 2:4, :])
        nc.vector.tensor_copy(out=w3_plane[:, HALF:H].rearrange("p (e m) -> p e m", e=2),
                              in_=w3_raw_plane[:].rearrange("p (m t) -> p t m", t=4)[:, 2:4, :])

        banks = {}

        def products(t, lo, hi):
            for name in ("b1", "b2", "b3"):
                bank = psum.tile([P, BANK], F32, name=name)
                banks[name, lo] = bank
                for at in range(lo, hi, P):
                    picked = slice(at, at + P)
                    for a in range(PASSES):
                        if name == "b3":
                            cols = slice(P * t, P * (t + 1))
                            codes, plane = w3c[:, a, cols], w3_plane[4 * a :, cols]
                        else:
                            slot = 2 * a + (name == "b2")
                            cols = slice(P * slot, P * (slot + 1))
                            codes, plane = w12c[:, cols], w_plane[:, cols]
                        nc.tensor.matmul_mx(
                            out=bank[:, at - lo : at - lo + P],
                            lhsT=v[a][:, picked].bitcast(FP8X4), lhsT_scale=v_plane[4 * a :, picked],
                            rhs=codes.bitcast(FP8X4), rhs_scale=plane,
                            start=(a == 0), stop=(a == PASSES - 1))

        def entries(t, lo, hi):
            width = hi - lo
            nc.scalar.copy(out=spare[:, lo:hi], in_=banks["b1", lo][:, 0:width])
            nc.scalar.copy(out=b3s[:, lo:hi], in_=banks["b3", lo][:, 0:width])
            nc.vector.tensor_tensor(mh[:, lo:hi], banks["b2", lo][:, 0:width], spare[:, lo:hi], ALU.max)
            turned = psum.tile([P, BANK], F32, name="turned")
            for at in range(lo, hi, P):
                cols = slice(at, at + P)
                place = turned[:, at - lo : at - lo + P]
                nc.tensor.matmul(place, lhsT=b3s[:, cols], rhs=ident[:], is_transpose=True, start=True, stop=False)
                nc.tensor.matmul(place, lhsT=mh[:, cols], rhs=ident[:], is_transpose=True, start=False, stop=True)
            scale = gain_ab[:, t : t + 1] if t < 2 else gain_cd[:, t - 2 : t - 1]
            nc.scalar.activation(out=mh[:, lo:hi], in_=turned[:, 0:width], func=ACT.Copy, scale=scale)

        def put(t, lo, hi):
            places = lists[1][:, lo // 16 : hi // 16]
            nc.vector.tensor_tensor(pages[t][:].indirect(places), mh[:, lo:hi], wgs_of[t][:, lo:hi], ALU.mult)

        def fetch_pairs(t):
            nc.vector.tensor_copy(first[:], pages[t][:].indirect(lists[2][:]))
            nc.vector.tensor_copy(second, pages[t][:].indirect(lists[3][:]))
            nc.vector.tensor_tensor(pages[t][:].indirect(lists[3][:]), first[:], second, ALU.add)

        def put_larger(t):
            if t < 3:
                larger = spare[:, S // 4 : S // 4 + PAIRS]
            else:
                larger = planes3[:, 0, T2 // 2 :].bitcast(F32)
            nc.vector.tensor_tensor(larger, first[:], second, ALU.max)
            nc.vector.tensor_copy(pages[t][:].indirect(lists[2][:]), larger)

        def round_ctx(piece):
            raw = load_piece(ctx, 0, PIECE * piece)
            c, at = divmod(PIECE * piece, OUT_COLS)
            nc.scalar.copy(out=last_in[c][:, 1, at : at + PIECE, :].rearrange("p (q i) j -> p q j i", i=4),
                           in_=raw[:].rearrange("p j (q i) -> p q j i", i=4))

        def round_page(t):
            if t < 2:
                nc.scalar.copy(out=rounded[:], in_=pages[t][:])
                for e in range(2):
                    nc.scalar.dma_start(out=planes3[64 * t : 64 * (t + 1), e, :], in_=rounded[e:P:2, :])
            else:
                nc.scalar.copy(out=planes3[:, 2, :], in_=pages[t][:])

        for span in SLICES[0]:
            products(0, *span)
            entries(0, *span)
        for slot in range(4):
            round_ab(nc.scalar.copy, w_in_b[:].bitcast(BF16), raw1[slot], slot)
        for slot in range(4):
            round_cd(raw0[slot], slot, 0)
        for slot in range(4):
            round_cd(raw1[slot], slot, 1)
        nc.scalar.copy(out=w5_in[:].rearrange("p (q i j) -> p q j i", i=4, j=4),
                       in_=w5_raw[:].rearrange("p j (q i) -> p q j i", i=4))
        sources = {1: w_in_b[:].bitcast(BF16), 2: w_in_cd[:, 0, :], 3: w_in_cd[:, 1, :]}
        quantise_w(sources[1], 0, 4 * P)
        for span in SLICES[1]:
            products(1, *span)

        for t in range(4):
            for span in SLICES[t]:
                put(t, *span)
            fetch_pairs(t)
            if t < 3:
                for span in SLICES[t + 1]:
                    entries(t + 1, *span)
            if t < 2:
                quantise_w(sources[t + 2], 0, 4 * P)
                for span in SLICES[t + 2]:
                    products(t + 2, *span)
            put_larger(t)
            if t < 3:
                round_page(t)
            if t == 0:
                for piece in range(4):
                    round_ctx(piece)
                wgs_of[2] = ring.tile([P, S], F32, name="dealt")
                load_wgs(wgs_of[2], 2, 0, S)
                load_page(2)
            if t == 1:
                nc.vector.quantize_mx(out=w5c[:].bitcast(FP8X4), scales=w_plane[4:, 0:N], in_=w5_in[:])
                for piece in range(4, 8):
                    round_ctx(piece)
                load_page(3)
                nc.sync.dma_start(out=w4c[:].bitcast(I32), in_=w4_words[0].bitcast(I32))
                wgs_of[3] = ring.tile([P, S], F32, name="dealt")
                load_wgs(wgs_of[3], 3, 0, S)
            if t == 2:
                for c in range(T2 // OUT_COLS):
                    cols = slice(OUT_COLS * c, OUT_COLS * (c + 1))
                    nc.scalar.copy(out=last_in[c][:, 0, :, 0:3], in_=planes3[:, :, cols].rearrange("p t c -> p c t"))

        tags = ("b1", "b2", "b3", "turned")
        chunks = T2 // OUT_COLS

        def round_last(copy, c):
            copy(out=last_in[c][:, 0, :, 3], in_=pages[3][:, OUT_COLS * c : OUT_COLS * (c + 1)])

        for c in range(chunks - SCALAR_CHUNKS, chunks):
            round_last(nc.scalar.copy, c)
        round_last(nc.vector.tensor_copy, 0)
        for c in range(chunks):
            if c + 1 < chunks - SCALAR_CHUNKS:
                round_last(nc.vector.tensor_copy, c + 1)
            codes = ring.tile([P, 2 * OUT_COLS], U32, name="codes", align_bytes=64, bufs=4)
            plane = ring.tile([P, 2 * OUT_COLS], U8, name="plane", align_bytes=64, bufs=4)
            nc.vector.quantize_mx(out=codes[:].bitcast(FP8X4), scales=plane[:],
                                  in_=last_in[c][:].rearrange("p s c j -> p (s c j)"))
            y = psum.tile([P, N // P, OUT_COLS], F32, name=tags[c % 4])
            for n in range(N // P):
                nc.tensor.matmul_mx(out=y[:, n, :], lhsT=w5c[:, P * n : P * (n + 1)].bitcast(FP8X4),
                                    lhsT_scale=w_plane[4:, P * n : P * (n + 1)],
                                    rhs=codes[:, OUT_COLS:].bitcast(FP8X4), rhs_scale=plane[:, OUT_COLS:],
                                    start=True, stop=False)
                nc.tensor.matmul_mx(out=y[:, n, :], lhsT=w4c[:, 2 * P * n : 2 * P * (n + 1)].bitcast(FP4X4),
                                    lhsT_scale=w4_plane[:, P * n : P * (n + 1)],
                                    rhs=codes[:, 0:OUT_COLS].bitcast(FP8X4), rhs_scale=plane[:, 0:OUT_COLS],
                                    start=False, stop=True)
            score = raws.tile([P, N // P, OUT_COLS], F32, name="raw", align_bytes=64)
            nc.scalar.activation(out=score[:], in_=y[:], func=ACT.Tanh)
            cols = slice(OUT_COLS * c, OUT_COLS * (c + 1))
            nc.sync.dma_start(out=out[:, cols].rearrange("(n p) c -> p n c", p=P), in_=score[:])
